import numpy as np
import ml_dtypes


def mxq(x, axis, fmt="e4m3"):
    dtype, down = {"e4m3": (ml_dtypes.float8_e4m3fn, 7), "e5m2": (ml_dtypes.float8_e5m2, 14)}[fmt]
    v = np.moveaxis(np.asarray(x, np.float32).astype(ml_dtypes.bfloat16).astype(np.float64), axis, -1)
    blocks = v.reshape(v.shape[:-1] + (-1, 32))
    amax = np.abs(blocks).max(-1, keepdims=True)
    byte = np.maximum(np.where(amax > 0, np.frexp(amax)[1] - 1 + 127, 0) - down, 1)
    scale = np.exp2(byte - 127.0)
    codes = (blocks / scale).astype(np.float32).astype(dtype).astype(np.float64)
    return np.moveaxis((codes * scale).reshape(v.shape), -1, axis)


WIDE = False


def mx_kscale(k):
    if not WIDE:
        return np.ones(k)
    levels = np.array([10, -10, 5, -5, 0])
    if k % 512:
        return np.exp2(np.random.permutation(np.resize(levels, k // 32))).repeat(32)
    a = np.empty((k // 512, 16))
    for p in range(k // 512):
        a[p, :8] = np.random.permutation(np.resize(levels, 8))
        for g in range(8):
            far = levels[np.abs(levels - a[p, g]) >= 10]
            a[p, g + 8] = far[np.random.randint(len(far))]
    return np.exp2(a.ravel()).repeat(32)


BF16 = ml_dtypes.bfloat16


def bf(x):
    return np.asarray(x, np.float32).astype(BF16)


def f64(x):
    return np.asarray(x).astype(np.float64)


E2M1 = np.array([0.0, 0.5, 1.0, 1.5, 2.0, 3.0, 4.0, 6.0, -0.0, -0.5, -1.0, -1.5, -2.0, -3.0, -4.0, -6.0])


def pack_weight(w, fmt):
    k, n = w.shape
    w = f64(bf(w)).reshape(k // 32, 32, n)
    amax = np.abs(w).max(1)
    if fmt == "e4m3":
        byte = np.frexp(amax)[1] - 1 + 127 - 7
    else:
        mant, ex = np.frexp(amax / 6.0)
        byte = np.where(mant > 0.5, ex, ex - 1) + 127
    byte = np.clip(np.where(amax > 0, byte, 1), 1, 254)
    scaled = (w * np.exp2(127.0 - byte)[:, None, :]).reshape(k, n).astype(np.float32)
    by_word = np.ascontiguousarray(scaled.reshape(k // 512, 128, 4, n).transpose(0, 1, 3, 2))
    if fmt == "e4m3":
        words = by_word.astype(ml_dtypes.float8_e4m3fn).view(np.uint8)
    else:
        c = by_word.astype(ml_dtypes.float4_e2m1fn).view(np.uint8) & 0xF
        words = c[..., 0::2] | (c[..., 1::2] << 4)
    return np.ascontiguousarray(words), np.ascontiguousarray(byte.astype(np.uint8).reshape(k // 512, 16, n))


def unpack_weight(words, scales, fmt):
    g, p, n, _ = words.shape
    if fmt == "e4m3":
        vals = np.ascontiguousarray(words).view(ml_dtypes.float8_e4m3fn).astype(np.float64)
    else:
        nib = np.empty((g, p, n, 4), np.uint8)
        nib[..., 0::2] = words & 0xF
        nib[..., 1::2] = words >> 4
        vals = E2M1[nib]
    vals = vals * np.repeat(np.exp2(scales.astype(np.float64) - 127.0), 8, axis=1)[..., None]
    return vals.transpose(0, 1, 3, 2).reshape(g * 512, n)
def pack4(w):
    words, scales = pack_weight(w, "e2m1")
    return words.reshape(words.shape[0], 128, -1), scales


def unpack4(words, scales):
    return unpack_weight(words.reshape(words.shape[0], 128, -1, 2), scales, "e2m1")


def planes(Y):
    n, m = Y.shape
    b = f64(bf(Y)).reshape(n // 32, 32, m)
    amax = np.abs(b).max(1)
    byte = np.clip(np.where(amax > 0, np.frexp(amax)[1] - 1 + 127 - 7, 1), 1, 254)
    codes = (b * np.exp2(127.0 - byte)[:, None, :]).reshape(n, m).astype(np.float32).astype(ml_dtypes.float8_e4m3fn).view(np.uint8)
    words = codes.reshape(n // 512, 128, 4, m).transpose(0, 1, 3, 2)
    return np.ascontiguousarray(words), np.ascontiguousarray(byte.astype(np.uint8).reshape(n // 512, 16, m))


B, D = 512, 1536


def sigmoid(v):
    return 1.0 / (1.0 + np.exp(-v))


def setup_inputs():
    s = mx_kscale(D)
    t = mx_kscale(D)
    x = bf(np.random.standard_normal((B, D)) * s[None, :])
    wg_words, wg_scales = pack4(np.random.standard_normal((D, D)) / np.sqrt(D) / s[:, None])
    wc1_words, wc1_scales = pack4(np.random.standard_normal((D, D)) / np.sqrt(D) / s[:, None])
    gm = bf((1.0 + 0.1 * np.random.standard_normal(D)) * t / s)
    wc2_words, wc2_scales = pack4(np.random.standard_normal((D, D)) / np.sqrt(D) / t[:, None])
    return {"x": x,
            "wg_words": wg_words, "wg_scales": wg_scales,
            "wc1_words": wc1_words, "wc1_scales": wc1_scales,
            "gm": gm,
            "wc2_words": wc2_words, "wc2_scales": wc2_scales}


def core(x, wg_words, wg_scales, wc1_words, wc1_scales, gm, wc2_words, wc2_scales):
    x = f64(x)
    xq = mxq(x, 1, "e4m3")
    xg = x * sigmoid(xq @ unpack4(wg_words, wg_scales))
    f1 = xq @ unpack4(wc1_words, wc1_scales)
    c1 = xg * f1 + x
    u = c1 * f64(gm)[None, :]
    f2 = mxq(u, 1, "e4m3") @ unpack4(wc2_words, wc2_scales)
    return xg * f2 + c1


def reference(x, wg_words, wg_scales, wc1_words, wc1_scales, gm, wc2_words, wc2_scales):
    R_out = core(x, wg_words, wg_scales, wc1_words, wc1_scales, gm, wc2_words, wc2_scales)
    words, scales = planes(R_out.T)
    return R_out, words, scales

@@ -1,0 +1,365 @@
+from contextlib import ExitStack
+
+import concourse.mybir as mybir
+from concourse.masks import make_identity
+
+B, D = 512, 1536
+FLOPS = 3 * 2 * B * D * D
+
+F32 = mybir.dt.float32
+BF16 = mybir.dt.bfloat16
+I32 = mybir.dt.int32
+U32 = mybir.dt.uint32
+U8 = mybir.dt.uint8
+FP8X4 = mybir.dt.float8_e4m3fn_x4
+FP4X4 = mybir.dt.float4_e2m1fn_x4
+ALU = mybir.AluOpType
+ACT = mybir.ActivationFunctionType
+
+P = 128
+G = D // 512
+TILES = B // P
+BLK = 512
+NB = TILES * G
+LAG = 4
+EARLY = 0
+REPEAT = 3
+
+
+def tile_gateddeepcrosstwolayer_x2_kernel(
+    tc, x, wg_words, wg_scales, wc1_words, wc1_scales, gm, wc2_words, wc2_scales, out_0, out_1, out_2
+):
+    nc = tc.nc
+    with ExitStack() as ctx:
+        keep = ctx.enter_context(tc.tile_pool(name="keep", bufs=1))
+        work = ctx.enter_context(tc.tile_pool(name="work", bufs=3))
+        psum = ctx.enter_context(tc.psum_pool(name="psum", bufs=2))
+        ctx.enter_context(tc.manual_schedule())
+
+        ident = keep.tile([P, P], F32, name="ident")
+        make_identity(nc, ident[:])
+        warm = keep.tile([P, 1], F32, name="warm")
+        nc.vector.memset(warm[:], 0.0)
+        nc.scalar.activation(out=warm[:], in_=warm[:], func=ACT.Sigmoid)
+
+        def scale_plane(name, engine):
+            t = keep.tile([P, G, D], U8, name=name, align_bytes=64)
+            engine.memset(t[:].rearrange("p g n -> p (g n)").bitcast(I32), 0)
+            return t
+
+        sg = scale_plane("sg", nc.vector)
+        sc1 = scale_plane("sc1", nc.vector)
+        sc2 = scale_plane("sc2", nc.gpsimd)
+
+        def load_scales(queue, t, scales):
+            for r in range(4):
+                queue.dma_start(
+                    out=t[r:P:32, :, :].bitcast(I32),
+                    in_=scales[:, r:16:4, :].rearrange("g q n -> q g n").bitcast(I32),
+                )
+
+        x_sb = [keep.tile([P, D], BF16, name="x%d" % i, align_bytes=64) for i in range(TILES)]
+
+        def load_x(i):
+            nc.sync.dma_start(out=x_sb[i][:], in_=x[P * i : P * (i + 1), :])
+
+        def load_w(name, words, j0, count):
+            t = keep.tile([P, G, 2 * BLK * count], U8, name="%s_%d" % (name, j0), align_bytes=64)
+            nc.sync.dma_start(
+                out=t[:].bitcast(I32),
+                in_=words[:, :, 2 * BLK * j0 : 2 * BLK * (j0 + count)].rearrange("g p n -> p g n").bitcast(I32),
+            )
+            return [(t, c) for c in range(count)]
+
+        load_x(0)
+        wg = load_w("wg", wg_words, 0, 1)
+        load_scales(nc.sync, sg, wg_scales)
+        wg += load_w("wg", wg_words, 1, 1)
+        wg += load_w("wg", wg_words, 2, 1)
+        wc1 = load_w("wc1", wc1_words, 0, 1)
+        load_scales(nc.sync, sc1, wc1_scales)
+        gm_sb = keep.tile([P, D], BF16, name="gm_sb", align_bytes=64)
+        nc.sync.dma_start(out=gm_sb[:], in_=gm.partition_broadcast(P))
+        wc1 += load_w("wc1", wc1_words, 1, 1)
+        load_x(1)
+        wc1 += load_w("wc1", wc1_words, 2, 1)
+        load_scales(nc.gpsimd, sc2, wc2_scales)
+        wc2 = load_w("wc2", wc2_words, 0, 3)
+        load_x(2)
+        load_x(3)
+
+        xc = [keep.tile([P, G, P], U32, name="xc%d" % i, align_bytes=64) for i in range(TILES)]
+        xs = [keep.tile([P, G, P], U8, name="xs%d" % i, align_bytes=64) for i in range(TILES)]
+        uc = [keep.tile([P, G, P], U32, name="uc%d" % i, align_bytes=64) for i in range(TILES)]
+        us = [keep.tile([P, G, P], U8, name="us%d" % i, align_bytes=64) for i in range(TILES)]
+        rc = [keep.tile([P, G, P], U32, name="rc%d" % i, align_bytes=64) for i in range(TILES)]
+        rs = keep.tile([P, G, B], U8, name="rs", align_bytes=64)
+        xgm = [keep.tile([P, D], F32, name="xgm%d" % i, align_bytes=64) for i in range(TILES)]
+
+        def mixed(ap):
+            return ap.rearrange("p (u q e) -> p q u e", u=2, e=2)
+
+        def natural(ap):
+            return ap.rearrange("p (q u e) -> p q u e", u=2, e=2)
+
+        def natural_as_mixed(ap):
+            return ap.rearrange("p (q u e) -> p u q e", u=2, e=2)
+
+        def mixed_run(ap):
+            return ap.rearrange("p (u q e) -> p u q e", u=2, e=2)
+
+        def xcols(n):
+            i, j = divmod(n, G)
+            return x_sb[i][:, BLK * j : BLK * (j + 1)]
+
+        def gcols(n):
+            j = n % G
+            return gm_sb[:, BLK * j : BLK * (j + 1)]
+
+        def xgm_cols(n):
+            i, j = divmod(n, G)
+            return xgm[i][:, BLK * j : BLK * (j + 1)]
+
+        gate_bank, first_bank, second_bank = {}, {}, {}
+        sig, m, u_sb, m2, r_sb, rb, grouped = {}, {}, {}, {}, {}, {}, {}
+
+        def mm(out, codes, scales, w, ws, j, start, stop):
+            tile, c = w[j]
+            for g in range(G):
+                nc.tensor.matmul_mx(
+                    out=out[:],
+                    lhsT=codes[:, g, :].bitcast(FP8X4),
+                    lhsT_scale=scales[:, g, :],
+                    rhs=tile[:, g, 2 * BLK * c : 2 * BLK * (c + 1)].bitcast(FP4X4),
+                    rhs_scale=ws[:, g, BLK * j : BLK * (j + 1)],
+                    start=start and g == 0,
+                    stop=stop and g == G - 1,
+                )
+
+        def gate(n):
+            i, j = divmod(n, G)
+            gate_bank[n] = psum.tile([P, BLK], F32, name="gb", tag="G")
+            mm(gate_bank[n], xc[i], xs[i], wg, sg, j, True, True)
+            sig[n] = work.tile([P, BLK], F32, name="sig", tag="sig", bufs=7)
+            nc.scalar.activation(out=sig[n][:], in_=gate_bank[n][:], func=ACT.Sigmoid)
+
+        def first(n):
+            i, j = divmod(n, G)
+            first_bank[n] = psum.tile([P, BLK], F32, name="fb", tag="F")
+            mm(first_bank[n], xc[i], xs[i], wc1, sc1, j, True, True)
+
+        def make_xgm(n):
+            nc.gpsimd.tensor_tensor(
+                out=mixed_run(xgm_cols(n)), in0=natural_as_mixed(xcols(n)), in1=natural_as_mixed(gcols(n)), op=ALU.mult
+            )
+
+        def early_xg(n):
+            nc.vector.tensor_tensor(out=sig[n][:], in0=sig[n][:], in1=xcols(n), op=ALU.mult)
+
+        def times_first(n):
+            m[n] = work.tile([P, BLK], F32, name="m", tag="m", bufs=7)
+            if n < EARLY:
+                nc.vector.tensor_tensor(out=m[n][:], in0=first_bank[n][:], in1=sig[n][:], op=ALU.mult)
+            else:
+                nc.vector.tensor_tensor(
+                    out=mixed_run(m[n][:]), in0=natural_as_mixed(first_bank[n][:]), in1=natural_as_mixed(sig[n][:]),
+                    op=ALU.mult,
+                )
+
+        def early_c1(n):
+            nc.vector.tensor_tensor(out=m[n][:], in0=m[n][:], in1=xcols(n), op=ALU.add)
+
+        def make_u(n):
+            u_sb[n] = work.tile([P, BLK], BF16, name="u", tag="u", bufs=4)
+            if n < EARLY:
+                nc.vector.tensor_tensor(
+                    out=mixed_run(u_sb[n][:]), in0=natural_as_mixed(m[n][:]), in1=natural_as_mixed(gcols(n)), op=ALU.mult
+                )
+            else:
+                nc.vector.scalar_tensor_tensor(
+                    out=u_sb[n][:], in0=m[n][:], scalar=1.0, in1=xgm_cols(n), op0=ALU.add, op1=ALU.mult
+                )
+
+        def transposes(items, tags=None, copies=None):
+            for a in range(0, len(items), 2):
+                pair = items[a : a + 2]
+                bank = psum.tile([P, 4 * P], F32, name="bank", tag=tags[a // 2] if tags else "T")
+                for h, (kind, n) in enumerate(pair):
+                    for w in range(2):
+                        if kind == "x":
+                            i, g = divmod(n, G)
+                            src = x_sb[i][:].bitcast(F32)[:, 256 * g + w : 256 * (g + 1) : 2]
+                        else:
+                            src = (u_sb if kind == "u" else rb)[n][:].bitcast(F32)
+                            if kind == "r" and n == NB - 1:
+                                src = src[:, w : 2 * P : 2]
+                            else:
+                                src = src[:, w * P : (w + 1) * P]
+                        col = (2 * h + w) * P
+                        nc.tensor.transpose(bank[:, col : col + P], src, ident[:])
+                for h, (kind, n) in enumerate(pair):
+                    t = work.tile([P, 4 * P], BF16, name="grouped", tag="grouped", bufs=6, align_bytes=64)
+                    copy = copies[a + h] if copies else nc.scalar.copy
+                    copy(
+                        out=t[:].bitcast(F32).rearrange("p (r u) -> p r u", u=2),
+                        in_=bank[:, 2 * P * h : 2 * P * (h + 1)].rearrange("p (u r) -> p r u", u=2),
+                    )
+                    grouped[kind, n] = t
+
+        def quantise(kind, n):
+            i, g = divmod(n, G)
+            codes = {"x": xc, "u": uc, "r": rc}[kind][i]
+            scales = rs[:, g, P * i : P * (i + 1)] if kind == "r" else (xs if kind == "x" else us)[i][:, g, :]
+            nc.vector.quantize_mx(out=codes[:, g, :].bitcast(FP8X4), scales=scales, in_=grouped[kind, n][:])
+            if kind == "r":
+                nc.sync.dma_start(
+                    out=out_1[g, :, P * i : P * (i + 1), :].rearrange("p m t -> p (m t)").bitcast(I32),
+                    in_=codes[:, g, :].bitcast(I32),
+                )
+
+        def second_start(b, tag="B"):
+            i, j = divmod(b, G)
+            second_bank[b] = psum.tile([P, BLK], F32, name="bb", tag=tag)
+            if b >= NB - REPEAT:
+                mm(second_bank[b], xc[i], xs[i], wc1, sc1, j, True, False)
+
+        def second_end(b):
+            i, j = divmod(b, G)
+            mm(second_bank[b], uc[i], us[i], wc2, sc2, j, b < NB - REPEAT, True)
+
+        def second(b):
+            second_start(b)
+            second_end(b)
+
+        def times_second(b):
+            m2[b] = work.tile([P, BLK], F32, name="m2", tag="m2", bufs=4)
+            nc.vector.tensor_tensor(out=m2[b][:], in0=second_bank[b][:], in1=sig[b][:], op=ALU.mult)
+
+        def add_first(b):
+            if EARLY <= b < NB - REPEAT:
+                nc.vector.tensor_tensor(out=natural(m2[b][:]), in0=natural(m2[b][:]), in1=mixed(m[b][:]), op=ALU.add)
+
+        def result(b):
+            i, j = divmod(b, G)
+            last = b == NB - 1
+            rb[b] = work.tile([P, BLK], BF16, name="rb", tag="rb", bufs=4)
+            if last:
+                nc.vector.scalar_tensor_tensor(
+                    out=rb[b][:], in0=m2[b][:], scalar=1.0, in1=xcols(b), op0=ALU.add, op1=ALU.mult
+                )
+            r_sb[b] = work.tile([P, BLK], F32, name="r", tag="r", bufs=4)
+            if b < EARLY:
+                nc.vector.tensor_tensor(out=r_sb[b][:], in0=m2[b][:], in1=m[b][:], op=ALU.add)
+            else:
+                nc.vector.scalar_tensor_tensor(
+                    out=r_sb[b][:], in0=m2[b][:], scalar=1.0, in1=xcols(b), op0=ALU.add, op1=ALU.mult
+                )
+            nc.sync.dma_start(out=out_0[P * i : P * (i + 1), BLK * j : BLK * (j + 1)], in_=r_sb[b][:])
+            if not last:
+                nc.scalar.activation(out=mixed_run(rb[b][:]), in_=natural_as_mixed(r_sb[b][:]), func=ACT.Copy)
+
+        transposes([("x", 0)], ("T",), (nc.vector.tensor_copy,))
+        transposes([("x", 1)], ("T",), (nc.scalar.copy,))
+        transposes([("x", 2)], ("B",), (nc.vector.tensor_copy,))
+        for n in range(G):
+            quantise("x", n)
+        for n in range(G):
+            gate(n)
+            if n < EARLY:
+                early_xg(n)
+            else:
+                make_xgm(n)
+        first(0)
+        times_first(0)
+        if EARLY > 0:
+            early_c1(0)
+        first(1)
+        make_u(0)
+        times_first(1)
+        transposes([("x", 3), ("x", 4)])
+        if EARLY > 1:
+            early_c1(1)
+        first(2)
+        quantise("x", 3)
+        make_u(1)
+        quantise("x", 4)
+        transposes([("x", 5), ("u", 0)])
+        times_first(2)
+        quantise("x", 5)
+        if EARLY > 2:
+            early_c1(2)
+        quantise("u", 0)
+        make_u(2)
+        for n in range(3, 6):
+            make_xgm(n)
+
+        for n in range(3, NB):
+            b = n - LAG
+            gate(n)
+            first(n)
+            items = [("u", n - 1)]
+            if n == 3:
+                items.insert(0, ("u", 1))
+            if 0 <= b - 2:
+                items.append(("r", b - 2))
+            if n + 3 < NB and n % G < 2:
+                items.append(("x", n + 3))
+            if n + 4 < NB and n % G == 1:
+                items.append(("x", n + 4))
+            transposes(items)
+            if 0 <= b:
+                second(b)
+            times_first(n)
+            if 0 <= b - 1:
+                result(b - 1)
+            make_u(n)
+            if 0 <= b:
+                times_second(b)
+            for kind, t in items:
+                if kind == "u":
+                    quantise(kind, t)
+            if 0 <= b:
+                add_first(b)
+            for kind, t in items:
+                if kind != "u":
+                    quantise(kind, t)
+            if n + 3 < NB:
+                make_xgm(n + 3)
+
+        second_start(9, "G")
+        second_start(10, "G")
+        transposes([("u", 11), ("r", 6)])
+        second(8)
+        second_start(11, "F")
+        result(7)
+        quantise("u", 11)
+        quantise("r", 6)
+        second_end(9)
+        times_second(8)
+        transposes([("r", 7)])
+        second_end(10)
+        second_end(11)
+        times_second(9)
+        add_first(8)
+        times_second(10)
+        result(8)
+        transposes([("r", 8)])
+        result(9)
+        quantise("r", 7)
+        times_second(11)
+        result(10)
+        transposes([("r", 9)])
+        result(11)
+        transposes([("r", 11)])
+        transposes([("r", 10)])
+        quantise("r", 8)
+        quantise("r", 9)
+        quantise("r", 10)
+        quantise("r", 11)
+
+        queues = (nc.sync, nc.scalar, nc.sync, nc.scalar)
+        for q in range(4):
+            queues[q].dma_start(
+                out=out_2[:, 4 * q : 4 * q + 4, :].rearrange("g q m -> q g m").bitcast(I32),
+                in_=rs[32 * q : 32 * q + 4, :, :].bitcast(I32),
+            )

@@ -24,6 +24,9 @@ NB = TILES * G
 LAG = 4
 EARLY = 0
 REPEAT = 3
+XG_BUFS = 6
+XGM_AT = {3: (4, 5), 4: (6,), 5: (7,), 6: (8,), 7: (9,), 8: (10,), 9: (11,)}
+XGM_G = {}
 
 
 def tile_gateddeepcrosstwolayer_x2_kernel(
@@ -36,6 +39,9 @@ def tile_gateddeepcrosstwolayer_x2_kernel(
         psum = ctx.enter_context(tc.psum_pool(name="psum", bufs=2))
         ctx.enter_context(tc.manual_schedule())
 
+        gm_rows = keep.tile([P, P], BF16, name="gm_rows", align_bytes=64)
+        nc.vector.memset(gm_rows[:], 0.0)
+        nc.gpsimd.dma_start(out=gm_rows[: D // P, :], in_=gm.rearrange("(c q) -> c q", q=P))
         ident = keep.tile([P, P], F32, name="ident")
         make_identity(nc, ident[:])
         warm = keep.tile([P, 1], F32, name="warm")
@@ -49,7 +55,9 @@ def tile_gateddeepcrosstwolayer_x2_kernel(
 
         sg = scale_plane("sg", nc.vector)
         sc1 = scale_plane("sc1", nc.vector)
-        sc2 = scale_plane("sc2", nc.gpsimd)
+        sc2 = scale_plane("sc2", nc.vector)
+        ident16 = keep.tile([P, P], BF16, name="ident16")
+        nc.vector.tensor_copy(out=ident16[:], in_=ident[:])
 
         def load_scales(queue, t, scales):
             for r in range(4):
@@ -74,16 +82,12 @@ def tile_gateddeepcrosstwolayer_x2_kernel(
         load_x(0)
         wg = load_w("wg", wg_words, 0, 1)
         load_scales(nc.sync, sg, wg_scales)
-        wg += load_w("wg", wg_words, 1, 1)
-        wg += load_w("wg", wg_words, 2, 1)
-        wc1 = load_w("wc1", wc1_words, 0, 1)
         load_scales(nc.sync, sc1, wc1_scales)
-        gm_sb = keep.tile([P, D], BF16, name="gm_sb", align_bytes=64)
-        nc.sync.dma_start(out=gm_sb[:], in_=gm.partition_broadcast(P))
-        wc1 += load_w("wc1", wc1_words, 1, 1)
+        wg += load_w("wg", wg_words, 1, 2)
+        wc1 = load_w("wc1", wc1_words, 0, 1)
         load_x(1)
-        wc1 += load_w("wc1", wc1_words, 2, 1)
-        load_scales(nc.gpsimd, sc2, wc2_scales)
+        wc1 += load_w("wc1", wc1_words, 1, 2)
+        load_scales(nc.sync, sc2, wc2_scales)
         wc2 = load_w("wc2", wc2_words, 0, 3)
         load_x(2)
         load_x(3)
@@ -94,7 +98,7 @@ def tile_gateddeepcrosstwolayer_x2_kernel(
         us = [keep.tile([P, G, P], U8, name="us%d" % i, align_bytes=64) for i in range(TILES)]
         rc = [keep.tile([P, G, P], U32, name="rc%d" % i, align_bytes=64) for i in range(TILES)]
         rs = keep.tile([P, G, B], U8, name="rs", align_bytes=64)
-        xgm = [keep.tile([P, D], F32, name="xgm%d" % i, align_bytes=64) for i in range(TILES)]
+        xgm = {}
 
         def mixed(ap):
             return ap.rearrange("p (u q e) -> p q u e", u=2, e=2)
@@ -115,10 +119,6 @@ def tile_gateddeepcrosstwolayer_x2_kernel(
         def gcols(n):
             j = n % G
             return gm_sb[:, BLK * j : BLK * (j + 1)]
-
-        def xgm_cols(n):
-            i, j = divmod(n, G)
-            return xgm[i][:, BLK * j : BLK * (j + 1)]
 
         gate_bank, first_bank, second_bank = {}, {}, {}
         sig, m, u_sb, m2, r_sb, rb, grouped = {}, {}, {}, {}, {}, {}, {}
@@ -148,9 +148,32 @@ def tile_gateddeepcrosstwolayer_x2_kernel(
             first_bank[n] = psum.tile([P, BLK], F32, name="fb", tag="F")
             mm(first_bank[n], xc[i], xs[i], wc1, sc1, j, True, True)
 
-        def make_xgm(n):
-            nc.gpsimd.tensor_tensor(
-                out=mixed_run(xgm_cols(n)), in0=natural_as_mixed(xcols(n)), in1=natural_as_mixed(gcols(n)), op=ALU.mult
+        gm_sb = keep.tile([P, D], BF16, name="gm_sb", align_bytes=64)
+
+        def spread_gm_columns():
+            bank = psum.tile([P, P], BF16, name="gbank", tag="F")
+            nc.tensor.transpose(bank[:], gm_rows[:], ident16[:])
+            gm_cols = keep.tile([P, P], BF16, name="gm_cols")
+            nc.scalar.copy(out=gm_cols[:], in_=bank[:])
+            return gm_cols
+
+        def spread_gm(gm_cols):
+            for first_col, count in ((0, 8), (8, 4)):
+                bank = psum.tile([P, 8 * P], BF16, name="gbank", tag="T")
+                for c in range(count):
+                    nc.tensor.transpose(
+                        bank[:, c * P : (c + 1) * P],
+                        gm_cols[:, first_col + c : first_col + c + 1].to_broadcast([P, P]),
+                        ident16[:],
+                    )
+                nc.scalar.copy(
+                    out=gm_sb[:, first_col * P : (first_col + count) * P], in_=bank[:, : count * P]
+                )
+
+        def make_xgm(n, engine):
+            xgm[n] = work.tile([P, BLK], F32, name="xgm", tag="xgv" if engine is nc.vector else "xgg", bufs=XG_BUFS if engine is nc.vector else 2)
+            engine.tensor_tensor(
+                out=mixed_run(xgm[n][:]), in0=natural_as_mixed(xcols(n)), in1=natural_as_mixed(gcols(n)), op=ALU.mult
             )
 
         def early_xg(n):
@@ -177,7 +200,7 @@ def tile_gateddeepcrosstwolayer_x2_kernel(
                 )
             else:
                 nc.vector.scalar_tensor_tensor(
-                    out=u_sb[n][:], in0=m[n][:], scalar=1.0, in1=xgm_cols(n), op0=ALU.add, op1=ALU.mult
+                    out=u_sb[n][:], in0=m[n][:], scalar=1.0, in1=xgm[n][:], op0=ALU.add, op1=ALU.mult
                 )
 
         def transposes(items, tags=None, copies=None):
@@ -258,93 +281,93 @@ def tile_gateddeepcrosstwolayer_x2_kernel(
             if not last:
                 nc.scalar.activation(out=mixed_run(rb[b][:]), in_=natural_as_mixed(r_sb[b][:]), func=ACT.Copy)
 
-        transposes([("x", 0)], ("T",), (nc.vector.tensor_copy,))
-        transposes([("x", 1)], ("T",), (nc.scalar.copy,))
+        gm_cols = spread_gm_columns()
+        spread_gm(gm_cols)
+        transposes([("x", 0)], ("B",), (nc.vector.tensor_copy,))
+        transposes([("x", 1)], ("G",), (nc.vector.tensor_copy,))
         transposes([("x", 2)], ("B",), (nc.vector.tensor_copy,))
         for n in range(G):
             quantise("x", n)
-        for n in range(G):
-            gate(n)
-            if n < EARLY:
-                early_xg(n)
-            else:
-                make_xgm(n)
+        gate(0)
+        make_xgm(0, nc.vector)
+        gate(1)
+        make_xgm(1, nc.vector)
+        gate(2)
+        make_xgm(2, nc.vector)
         first(0)
-        times_first(0)
-        if EARLY > 0:
-            early_c1(0)
-        first(1)
-        make_u(0)
-        times_first(1)
         transposes([("x", 3), ("x", 4)])
-        if EARLY > 1:
-            early_c1(1)
-        first(2)
+        transposes([("x", 5)])
+        make_xgm(3, nc.vector)
+        times_first(0)
+        first(1)
         quantise("x", 3)
-        make_u(1)
         quantise("x", 4)
-        transposes([("x", 5), ("u", 0)])
-        times_first(2)
+        make_u(0)
         quantise("x", 5)
-        if EARLY > 2:
-            early_c1(2)
+        times_first(1)
+        transposes([("u", 0)])
+        first(2)
+        make_u(1)
         quantise("u", 0)
-        make_u(2)
-        for n in range(3, 6):
-            make_xgm(n)
+        times_first(2)
 
-        for n in range(3, NB):
-            b = n - LAG
-            gate(n)
-            first(n)
-            items = [("u", n - 1)]
-            if n == 3:
+        for k in range(G, NB):
+            gate(k)
+            first(k)
+            make_u(k - 1)
+            for t in XGM_G.get(k, ()):
+                make_xgm(t, nc.gpsimd)
+            items = [("u", k - 1)]
+            if k == G:
                 items.insert(0, ("u", 1))
-            if 0 <= b - 2:
-                items.append(("r", b - 2))
-            if n + 3 < NB and n % G < 2:
-                items.append(("x", n + 3))
-            if n + 4 < NB and n % G == 1:
-                items.append(("x", n + 4))
+            if k >= LAG + 2:
+                items.append(("r", k - LAG - 2))
+            if k + 3 < NB and k % G < 2:
+                items.append(("x", k + 3))
+            if k + 4 < NB and k % G == 1:
+                items.append(("x", k + 4))
+            if k >= LAG:
+                second(k - LAG)
             transposes(items)
-            if 0 <= b:
-                second(b)
-            times_first(n)
-            if 0 <= b - 1:
-                result(b - 1)
-            make_u(n)
-            if 0 <= b:
+            b = k - LAG - 1
+            if b >= 0:
                 times_second(b)
-            for kind, t in items:
-                if kind == "u":
-                    quantise(kind, t)
-            if 0 <= b:
+            times_first(k)
+            for t in XGM_AT.get(k, ()):
+                make_xgm(t, nc.vector)
+            if b >= 0:
                 add_first(b)
             for kind, t in items:
-                if kind != "u":
+                if kind == "x":
                     quantise(kind, t)
-            if n + 3 < NB:
-                make_xgm(n + 3)
+            if b >= 0:
+                result(b)
+            for kind, t in items:
+                if kind != "x":
+                    quantise(kind, t)
 
         second_start(9, "G")
+        make_u(11)
         second_start(10, "G")
         transposes([("u", 11), ("r", 6)])
         second(8)
         second_start(11, "F")
-        result(7)
-        quantise("u", 11)
+        times_second(7)
         quantise("r", 6)
+        quantise("u", 11)
+        add_first(7)
         second_end(9)
         times_second(8)
-        transposes([("r", 7)])
+        result(7)
+        add_first(8)
         second_end(10)
+        transposes([("r", 7)])
         second_end(11)
         times_second(9)
-        add_first(8)
-        times_second(10)
         result(8)
-        transposes([("r", 8)])
+        times_second(10)
         result(9)
+        transposes([("r", 8)])
         quantise("r", 7)
         times_second(11)
         result(10)

@@ -25,7 +25,7 @@ LAG = 4
 EARLY = 0
 REPEAT = 3
 XG_BUFS = 6
-XGM_AT = {3: (4, 5), 4: (6,), 5: (7,), 6: (8,), 7: (9,), 8: (10,), 9: (11,)}
+XGM_AT = {4: (6,), 5: (7,), 6: (8,), 7: (9,), 8: (10,), 9: (11,)}
 XGM_G = {}
 
 
@@ -100,18 +100,6 @@ def tile_gateddeepcrosstwolayer_x2_kernel(
         rs = keep.tile([P, G, B], U8, name="rs", align_bytes=64)
         xgm = {}
 
-        def mixed(ap):
-            return ap.rearrange("p (u q e) -> p q u e", u=2, e=2)
-
-        def natural(ap):
-            return ap.rearrange("p (q u e) -> p q u e", u=2, e=2)
-
-        def natural_as_mixed(ap):
-            return ap.rearrange("p (q u e) -> p u q e", u=2, e=2)
-
-        def mixed_run(ap):
-            return ap.rearrange("p (u q e) -> p u q e", u=2, e=2)
-
         def xcols(n):
             i, j = divmod(n, G)
             return x_sb[i][:, BLK * j : BLK * (j + 1)]
@@ -173,7 +161,7 @@ def tile_gateddeepcrosstwolayer_x2_kernel(
         def make_xgm(n, engine):
             xgm[n] = work.tile([P, BLK], F32, name="xgm", tag="xgv" if engine is nc.vector else "xgg", bufs=XG_BUFS if engine is nc.vector else 2)
             engine.tensor_tensor(
-                out=mixed_run(xgm[n][:]), in0=natural_as_mixed(xcols(n)), in1=natural_as_mixed(gcols(n)), op=ALU.mult
+                out=xgm[n][:], in0=xcols(n), in1=gcols(n), op=ALU.mult
             )
 
         def early_xg(n):
@@ -185,7 +173,7 @@ def tile_gateddeepcrosstwolayer_x2_kernel(
                 nc.vector.tensor_tensor(out=m[n][:], in0=first_bank[n][:], in1=sig[n][:], op=ALU.mult)
             else:
                 nc.vector.tensor_tensor(
-                    out=mixed_run(m[n][:]), in0=natural_as_mixed(first_bank[n][:]), in1=natural_as_mixed(sig[n][:]),
+                    out=m[n][:], in0=first_bank[n][:], in1=sig[n][:],
                     op=ALU.mult,
                 )
 
@@ -196,7 +184,7 @@ def tile_gateddeepcrosstwolayer_x2_kernel(
             u_sb[n] = work.tile([P, BLK], BF16, name="u", tag="u", bufs=4)
             if n < EARLY:
                 nc.vector.tensor_tensor(
-                    out=mixed_run(u_sb[n][:]), in0=natural_as_mixed(m[n][:]), in1=natural_as_mixed(gcols(n)), op=ALU.mult
+                    out=u_sb[n][:], in0=m[n][:], in1=gcols(n), op=ALU.mult
                 )
             else:
                 nc.vector.scalar_tensor_tensor(
@@ -214,10 +202,7 @@ def tile_gateddeepcrosstwolayer_x2_kernel(
                             src = x_sb[i][:].bitcast(F32)[:, 256 * g + w : 256 * (g + 1) : 2]
                         else:
                             src = (u_sb if kind == "u" else rb)[n][:].bitcast(F32)
-                            if kind == "r" and n == NB - 1:
-                                src = src[:, w : 2 * P : 2]
-                            else:
-                                src = src[:, w * P : (w + 1) * P]
+                            src = src[:, w : 2 * P : 2]
                         col = (2 * h + w) * P
                         nc.tensor.transpose(bank[:, col : col + P], src, ident[:])
                 for h, (kind, n) in enumerate(pair):
@@ -260,7 +245,7 @@ def tile_gateddeepcrosstwolayer_x2_kernel(
 
         def add_first(b):
             if EARLY <= b < NB - REPEAT:
-                nc.vector.tensor_tensor(out=natural(m2[b][:]), in0=natural(m2[b][:]), in1=mixed(m[b][:]), op=ALU.add)
+                nc.vector.tensor_tensor(out=m2[b][:], in0=m2[b][:], in1=m[b][:], op=ALU.add)
 
         def result(b):
             i, j = divmod(b, G)
@@ -279,7 +264,7 @@ def tile_gateddeepcrosstwolayer_x2_kernel(
                 )
             nc.sync.dma_start(out=out_0[P * i : P * (i + 1), BLK * j : BLK * (j + 1)], in_=r_sb[b][:])
             if not last:
-                nc.scalar.activation(out=mixed_run(rb[b][:]), in_=natural_as_mixed(r_sb[b][:]), func=ACT.Copy)
+                nc.scalar.activation(out=rb[b][:], in_=r_sb[b][:], func=ACT.Copy)
 
         gm_cols = spread_gm_columns()
         spread_gm(gm_cols)
@@ -305,11 +290,13 @@ def tile_gateddeepcrosstwolayer_x2_kernel(
         make_u(0)
         quantise("x", 5)
         times_first(1)
+        make_xgm(4, nc.vector)
         transposes([("u", 0)])
         first(2)
         make_u(1)
         quantise("u", 0)
         times_first(2)
+        make_xgm(5, nc.vector)
 
         for k in range(G, NB):
             gate(k)
@@ -333,18 +320,18 @@ def tile_gateddeepcrosstwolayer_x2_kernel(
             if b >= 0:
                 times_second(b)
             times_first(k)
-            for t in XGM_AT.get(k, ()):
-                make_xgm(t, nc.vector)
             if b >= 0:
                 add_first(b)
+            for t in XGM_AT.get(k, ()):
+                make_xgm(t, nc.vector)
             for kind, t in items:
-                if kind == "x":
+                if kind != "u":
                     quantise(kind, t)
             if b >= 0:
                 result(b)
-            for kind, t in items:
-                if kind != "x":
-                    quantise(kind, t)
+            quantise("u", k - 1)
+            if k == G:
+                quantise("u", 1)
 
         second_start(9, "G")
         make_u(11)

@@ -20,13 +20,9 @@ P = 128
 G = D // 512
 TILES = B // P
 BLK = 512
-NB = TILES * G
-LAG = 4
-EARLY = 0
-REPEAT = 3
-XG_BUFS = 6
-XGM_AT = {4: (6,), 5: (7,), 6: (8,), 7: (9,), 8: (10,), 9: (11,)}
-XGM_G = {}
+HALVES = TILES // 2
+STEPS = HALVES * G
+REPEAT = 2
 
 
 def tile_gateddeepcrosstwolayer_x2_kernel(
@@ -48,28 +44,28 @@ def tile_gateddeepcrosstwolayer_x2_kernel(
         nc.vector.memset(warm[:], 0.0)
         nc.scalar.activation(out=warm[:], in_=warm[:], func=ACT.Sigmoid)
 
-        def scale_plane(name, engine):
+        def scale_plane(name):
             t = keep.tile([P, G, D], U8, name=name, align_bytes=64)
-            engine.memset(t[:].rearrange("p g n -> p (g n)").bitcast(I32), 0)
+            nc.vector.memset(t[:].rearrange("p g n -> p (g n)").bitcast(I32), 0)
             return t
 
-        sg = scale_plane("sg", nc.vector)
-        sc1 = scale_plane("sc1", nc.vector)
-        sc2 = scale_plane("sc2", nc.vector)
+        sg = scale_plane("sg")
+        sc1 = scale_plane("sc1")
+        sc2 = scale_plane("sc2")
         ident16 = keep.tile([P, P], BF16, name="ident16")
         nc.vector.tensor_copy(out=ident16[:], in_=ident[:])
 
-        def load_scales(queue, t, scales):
+        def load_scales(t, scales):
             for r in range(4):
-                queue.dma_start(
+                nc.sync.dma_start(
                     out=t[r:P:32, :, :].bitcast(I32),
                     in_=scales[:, r:16:4, :].rearrange("g q n -> q g n").bitcast(I32),
                 )
 
-        x_sb = [keep.tile([P, D], BF16, name="x%d" % i, align_bytes=64) for i in range(TILES)]
+        x_sb = keep.tile([P, TILES, D], BF16, name="x_sb", align_bytes=64)
 
         def load_x(i):
-            nc.sync.dma_start(out=x_sb[i][:], in_=x[P * i : P * (i + 1), :])
+            nc.sync.dma_start(out=x_sb[:, i, :], in_=x[P * i : P * (i + 1), :])
 
         def load_w(name, words, j0, count):
             t = keep.tile([P, G, 2 * BLK * count], U8, name="%s_%d" % (name, j0), align_bytes=64)
@@ -81,61 +77,21 @@ def tile_gateddeepcrosstwolayer_x2_kernel(
 
         load_x(0)
         wg = load_w("wg", wg_words, 0, 1)
-        load_scales(nc.sync, sg, wg_scales)
-        load_scales(nc.sync, sc1, wc1_scales)
-        wg += load_w("wg", wg_words, 1, 2)
+        load_scales(sg, wg_scales)
+        load_scales(sc1, wc1_scales)
         wc1 = load_w("wc1", wc1_words, 0, 1)
         load_x(1)
-        wc1 += load_w("wc1", wc1_words, 1, 2)
-        load_scales(nc.sync, sc2, wc2_scales)
-        wc2 = load_w("wc2", wc2_words, 0, 3)
+        wg += load_w("wg", wg_words, 1, 1)
+        wc1 += load_w("wc1", wc1_words, 1, 1)
         load_x(2)
         load_x(3)
+        wg += load_w("wg", wg_words, 2, 1)
+        wc1 += load_w("wc1", wc1_words, 2, 1)
+        load_scales(sc2, wc2_scales)
+        wc2 = load_w("wc2", wc2_words, 0, 3)
 
-        xc = [keep.tile([P, G, P], U32, name="xc%d" % i, align_bytes=64) for i in range(TILES)]
-        xs = [keep.tile([P, G, P], U8, name="xs%d" % i, align_bytes=64) for i in range(TILES)]
-        uc = [keep.tile([P, G, P], U32, name="uc%d" % i, align_bytes=64) for i in range(TILES)]
-        us = [keep.tile([P, G, P], U8, name="us%d" % i, align_bytes=64) for i in range(TILES)]
-        rc = [keep.tile([P, G, P], U32, name="rc%d" % i, align_bytes=64) for i in range(TILES)]
-        rs = keep.tile([P, G, B], U8, name="rs", align_bytes=64)
-        xgm = {}
-
-        def xcols(n):
-            i, j = divmod(n, G)
-            return x_sb[i][:, BLK * j : BLK * (j + 1)]
-
-        def gcols(n):
-            j = n % G
-            return gm_sb[:, BLK * j : BLK * (j + 1)]
-
-        gate_bank, first_bank, second_bank = {}, {}, {}
-        sig, m, u_sb, m2, r_sb, rb, grouped = {}, {}, {}, {}, {}, {}, {}
-
-        def mm(out, codes, scales, w, ws, j, start, stop):
-            tile, c = w[j]
-            for g in range(G):
-                nc.tensor.matmul_mx(
-                    out=out[:],
-                    lhsT=codes[:, g, :].bitcast(FP8X4),
-                    lhsT_scale=scales[:, g, :],
-                    rhs=tile[:, g, 2 * BLK * c : 2 * BLK * (c + 1)].bitcast(FP4X4),
-                    rhs_scale=ws[:, g, BLK * j : BLK * (j + 1)],
-                    start=start and g == 0,
-                    stop=stop and g == G - 1,
-                )
-
-        def gate(n):
-            i, j = divmod(n, G)
-            gate_bank[n] = psum.tile([P, BLK], F32, name="gb", tag="G")
-            mm(gate_bank[n], xc[i], xs[i], wg, sg, j, True, True)
-            sig[n] = work.tile([P, BLK], F32, name="sig", tag="sig", bufs=7)
-            nc.scalar.activation(out=sig[n][:], in_=gate_bank[n][:], func=ACT.Sigmoid)
-
-        def first(n):
-            i, j = divmod(n, G)
-            first_bank[n] = psum.tile([P, BLK], F32, name="fb", tag="F")
-            mm(first_bank[n], xc[i], xs[i], wc1, sc1, j, True, True)
-
+        xc, uc, rc = [keep.tile([P, G, B], U32, name=n, align_bytes=64) for n in ("xc", "uc", "rc")]
+        xs, us, rs = [keep.tile([P, G, B], U8, name=n, align_bytes=64) for n in ("xs", "us", "rs")]
         gm_sb = keep.tile([P, D], BF16, name="gm_sb", align_bytes=64)
 
         def spread_gm_columns():
@@ -158,218 +114,266 @@ def tile_gateddeepcrosstwolayer_x2_kernel(
                     out=gm_sb[:, first_col * P : (first_col + count) * P], in_=bank[:, : count * P]
                 )
 
-        def make_xgm(n, engine):
-            xgm[n] = work.tile([P, BLK], F32, name="xgm", tag="xgv" if engine is nc.vector else "xgg", bufs=XG_BUFS if engine is nc.vector else 2)
-            engine.tensor_tensor(
-                out=xgm[n][:], in0=xcols(n), in1=gcols(n), op=ALU.mult
+        gate_bank, first_bank, second_bank = {}, {}, {}
+        sig, m, u_sb, m2, r_sb, rb, xgm, grouped = {}, {}, {}, {}, {}, {}, {}, {}
+
+        def x_of(p, t=None):
+            h, j = divmod(p, G)
+            c = slice(BLK * j, BLK * (j + 1))
+            return x_sb[:, 2 * h : 2 * h + 2, c] if t is None else x_sb[:, 2 * h + t, c]
+
+        def mm(out, codes, scales, p, t, w, ws, start, stop):
+            h, j = divmod(p, G)
+            tok = slice(P * (2 * h + t), P * (2 * h + t + 1))
+            tile, c = w[j]
+            for g in range(G):
+                nc.tensor.matmul_mx(
+                    out=out[:],
+                    lhsT=codes[:, g, tok].bitcast(FP8X4),
+                    lhsT_scale=scales[:, g, tok],
+                    rhs=tile[:, g, 2 * BLK * c : 2 * BLK * (c + 1)].bitcast(FP4X4),
+                    rhs_scale=ws[:, g, BLK * j : BLK * (j + 1)],
+                    start=start and g == 0,
+                    stop=stop and g == G - 1,
+                )
+
+        def gate(p, t):
+            gate_bank[p, t] = psum.tile([P, BLK], F32, name="gb", tag="G")
+            mm(gate_bank[p, t], xc, xs, p, t, wg, sg, True, True)
+            if t == 0:
+                sig[p] = work.tile([P, 2, BLK], F32, name="sig", tag="sig", bufs=6)
+            nc.scalar.activation(out=sig[p][:, t, :], in_=gate_bank[p, t][:], func=ACT.Sigmoid)
+
+        def first(p, t):
+            first_bank[p, t] = psum.tile([P, BLK], F32, name="fb", tag="F")
+            mm(first_bank[p, t], xc, xs, p, t, wc1, sc1, True, True)
+
+        def make_xgm(p, t=None, engine=None):
+            j = p % G
+            if p not in xgm:
+                xgm[p] = work.tile([P, 2, BLK], F32, name="xgm", tag="xgm", bufs=6)
+            g = gm_sb[:, BLK * j : BLK * (j + 1)]
+            (engine or nc.vector).tensor_tensor(
+                out=xgm[p][:] if t is None else xgm[p][:, t, :],
+                in0=x_of(p, t),
+                in1=g.unsqueeze(1).to_broadcast([P, 2, BLK]) if t is None else g,
+                op=ALU.mult,
             )
 
-        def early_xg(n):
-            nc.vector.tensor_tensor(out=sig[n][:], in0=sig[n][:], in1=xcols(n), op=ALU.mult)
+        def times_first(p, t):
+            if t == 0:
+                m[p] = work.tile([P, 2, BLK], F32, name="m", tag="m", bufs=5)
+            nc.vector.tensor_tensor(out=m[p][:, t, :], in0=first_bank[p, t][:], in1=sig[p][:, t, :], op=ALU.mult)
 
-        def times_first(n):
-            m[n] = work.tile([P, BLK], F32, name="m", tag="m", bufs=7)
-            if n < EARLY:
-                nc.vector.tensor_tensor(out=m[n][:], in0=first_bank[n][:], in1=sig[n][:], op=ALU.mult)
-            else:
-                nc.vector.tensor_tensor(
-                    out=m[n][:], in0=first_bank[n][:], in1=sig[n][:],
-                    op=ALU.mult,
-                )
+        def make_u(p):
+            u_sb[p] = work.tile([P, 2, BLK], BF16, name="u", tag="u", bufs=2)
+            nc.vector.scalar_tensor_tensor(
+                out=u_sb[p][:], in0=m[p][:], scalar=1.0, in1=xgm[p][:], op0=ALU.add, op1=ALU.mult
+            )
 
-        def early_c1(n):
-            nc.vector.tensor_tensor(out=m[n][:], in0=m[n][:], in1=xcols(n), op=ALU.add)
+        def transposes(kind, p, tiles=(0, 1), tag="T", copy=nc.scalar.copy):
+            bank = psum.tile([P, 4 * P], F32, name="bank", tag=tag)
+            n = len(tiles)
+            for k, t in enumerate(tiles):
+                src = x_of(p, t) if kind == "x" else (u_sb if kind == "u" else rb)[p][:, t, :]
+                for w in range(2):
+                    col = (2 * k + w) * P
+                    nc.tensor.transpose(bank[:, col : col + P], src.bitcast(F32)[:, w : 2 * P : 2], ident[:])
+            g = work.tile([P, 8 * P], BF16, name="grouped", tag="grouped", bufs=5, align_bytes=64)
+            copy(
+                out=g[:, : 4 * P * n].bitcast(F32).rearrange("p (k r u) -> p k r u", k=n, u=2),
+                in_=bank[:, : 2 * P * n].rearrange("p (k u r) -> p k r u", k=n, u=2),
+            )
+            grouped[kind, p, tiles] = g
 
-        def make_u(n):
-            u_sb[n] = work.tile([P, BLK], BF16, name="u", tag="u", bufs=4)
-            if n < EARLY:
-                nc.vector.tensor_tensor(
-                    out=u_sb[n][:], in0=m[n][:], in1=gcols(n), op=ALU.mult
-                )
-            else:
-                nc.vector.scalar_tensor_tensor(
-                    out=u_sb[n][:], in0=m[n][:], scalar=1.0, in1=xgm[n][:], op0=ALU.add, op1=ALU.mult
-                )
-
-        def transposes(items, tags=None, copies=None):
-            for a in range(0, len(items), 2):
-                pair = items[a : a + 2]
-                bank = psum.tile([P, 4 * P], F32, name="bank", tag=tags[a // 2] if tags else "T")
-                for h, (kind, n) in enumerate(pair):
-                    for w in range(2):
-                        if kind == "x":
-                            i, g = divmod(n, G)
-                            src = x_sb[i][:].bitcast(F32)[:, 256 * g + w : 256 * (g + 1) : 2]
-                        else:
-                            src = (u_sb if kind == "u" else rb)[n][:].bitcast(F32)
-                            src = src[:, w : 2 * P : 2]
-                        col = (2 * h + w) * P
-                        nc.tensor.transpose(bank[:, col : col + P], src, ident[:])
-                for h, (kind, n) in enumerate(pair):
-                    t = work.tile([P, 4 * P], BF16, name="grouped", tag="grouped", bufs=6, align_bytes=64)
-                    copy = copies[a + h] if copies else nc.scalar.copy
-                    copy(
-                        out=t[:].bitcast(F32).rearrange("p (r u) -> p r u", u=2),
-                        in_=bank[:, 2 * P * h : 2 * P * (h + 1)].rearrange("p (u r) -> p r u", u=2),
-                    )
-                    grouped[kind, n] = t
-
-        def quantise(kind, n):
-            i, g = divmod(n, G)
-            codes = {"x": xc, "u": uc, "r": rc}[kind][i]
-            scales = rs[:, g, P * i : P * (i + 1)] if kind == "r" else (xs if kind == "x" else us)[i][:, g, :]
-            nc.vector.quantize_mx(out=codes[:, g, :].bitcast(FP8X4), scales=scales, in_=grouped[kind, n][:])
+        def quantise(kind, p, tiles=(0, 1)):
+            h, j = divmod(p, G)
+            codes, scales = {"x": (xc, xs), "u": (uc, us), "r": (rc, rs)}[kind]
+            n = len(tiles)
+            tok = slice(P * (2 * h + tiles[0]), P * (2 * h + tiles[0] + n))
+            nc.vector.quantize_mx(
+                out=codes[:, j, tok].bitcast(FP8X4),
+                scales=scales[:, j, tok],
+                in_=grouped[kind, p, tiles][:, : 4 * P * n],
+            )
             if kind == "r":
                 nc.sync.dma_start(
-                    out=out_1[g, :, P * i : P * (i + 1), :].rearrange("p m t -> p (m t)").bitcast(I32),
-                    in_=codes[:, g, :].bitcast(I32),
+                    out=out_1[j, :, tok, :].rearrange("p m t -> p (m t)").bitcast(I32),
+                    in_=rc[:, j, tok].bitcast(I32),
                 )
 
-        def second_start(b, tag="B"):
-            i, j = divmod(b, G)
-            second_bank[b] = psum.tile([P, BLK], F32, name="bb", tag=tag)
-            if b >= NB - REPEAT:
-                mm(second_bank[b], xc[i], xs[i], wc1, sc1, j, True, False)
+        def store_scales():
+            queues = (nc.sync, nc.scalar)
+            for q in range(4):
+                queues[q % 2].dma_start(
+                    out=out_2[:, 4 * q : 4 * q + 4, :].rearrange("g q m -> q g m").bitcast(I32),
+                    in_=rs[32 * q : 32 * q + 4, :, :].bitcast(I32),
+                )
 
-        def second_end(b):
-            i, j = divmod(b, G)
-            mm(second_bank[b], uc[i], us[i], wc2, sc2, j, b < NB - REPEAT, True)
+        def repeated(p):
+            return p >= STEPS - REPEAT
 
-        def second(b):
-            second_start(b)
-            second_end(b)
+        def second_start(p, t, tag="B"):
+            second_bank[p, t] = psum.tile([P, BLK], F32, name="bb", tag=tag)
+            if repeated(p):
+                mm(second_bank[p, t], xc, xs, p, t, wc1, sc1, True, False)
 
-        def times_second(b):
-            m2[b] = work.tile([P, BLK], F32, name="m2", tag="m2", bufs=4)
-            nc.vector.tensor_tensor(out=m2[b][:], in0=second_bank[b][:], in1=sig[b][:], op=ALU.mult)
+        def second_end(p, t):
+            mm(second_bank[p, t], uc, us, p, t, wc2, sc2, not repeated(p), True)
 
-        def add_first(b):
-            if EARLY <= b < NB - REPEAT:
-                nc.vector.tensor_tensor(out=m2[b][:], in0=m2[b][:], in1=m[b][:], op=ALU.add)
+        def times_second(p, t):
+            if t == 0:
+                m2[p] = work.tile([P, 2, BLK], F32, name="m2", tag="m2", bufs=3)
+            nc.vector.tensor_tensor(out=m2[p][:, t, :], in0=second_bank[p, t][:], in1=sig[p][:, t, :], op=ALU.mult)
 
-        def result(b):
-            i, j = divmod(b, G)
-            last = b == NB - 1
-            rb[b] = work.tile([P, BLK], BF16, name="rb", tag="rb", bufs=4)
-            if last:
+        def add_first(p):
+            if not repeated(p):
+                nc.vector.tensor_tensor(out=m2[p][:], in0=m2[p][:], in1=m[p][:], op=ALU.add)
+
+        def result(p, t=None, own_bf16=False):
+            h, j = divmod(p, G)
+            if p not in r_sb:
+                r_sb[p] = work.tile([P, 2, BLK], F32, name="r", tag="r", bufs=3)
+                rb[p] = work.tile([P, 2, BLK], BF16, name="rb", tag="rb", bufs=3)
+            part = (lambda a: a[:]) if t is None else (lambda a: a[:, t, :])
+            for a in [rb[p], r_sb[p]] if own_bf16 else [r_sb[p]]:
                 nc.vector.scalar_tensor_tensor(
-                    out=rb[b][:], in0=m2[b][:], scalar=1.0, in1=xcols(b), op0=ALU.add, op1=ALU.mult
+                    out=part(a), in0=part(m2[p]), scalar=1.0, in1=x_of(p, t), op0=ALU.add, op1=ALU.mult
                 )
-            r_sb[b] = work.tile([P, BLK], F32, name="r", tag="r", bufs=4)
-            if b < EARLY:
-                nc.vector.tensor_tensor(out=r_sb[b][:], in0=m2[b][:], in1=m[b][:], op=ALU.add)
+            c = slice(BLK * j, BLK * (j + 1))
+            if t is None:
+                dst = out_0[2 * P * h : 2 * P * (h + 1), c].rearrange("(t p) n -> p t n", t=2)
             else:
-                nc.vector.scalar_tensor_tensor(
-                    out=r_sb[b][:], in0=m2[b][:], scalar=1.0, in1=xcols(b), op0=ALU.add, op1=ALU.mult
-                )
-            nc.sync.dma_start(out=out_0[P * i : P * (i + 1), BLK * j : BLK * (j + 1)], in_=r_sb[b][:])
-            if not last:
-                nc.scalar.activation(out=rb[b][:], in_=r_sb[b][:], func=ACT.Copy)
+                dst = out_0[P * (2 * h + t) : P * (2 * h + t + 1), c]
+            nc.sync.dma_start(out=dst, in_=part(r_sb[p]))
+
+        def round_result(p, t=None):
+            part = (lambda a: a[:]) if t is None else (lambda a: a[:, t, :])
+            nc.scalar.copy(out=part(rb[p]), in_=part(r_sb[p]))
 
         gm_cols = spread_gm_columns()
+        for p, tag, copy in ((0, "B", nc.vector.tensor_copy), (1, "G", nc.scalar.copy), (2, "B", nc.vector.tensor_copy)):
+            transposes("x", p, (0,), tag, copy)
         spread_gm(gm_cols)
-        transposes([("x", 0)], ("B",), (nc.vector.tensor_copy,))
-        transposes([("x", 1)], ("G",), (nc.vector.tensor_copy,))
-        transposes([("x", 2)], ("B",), (nc.vector.tensor_copy,))
-        for n in range(G):
-            quantise("x", n)
-        gate(0)
-        make_xgm(0, nc.vector)
-        gate(1)
-        make_xgm(1, nc.vector)
-        gate(2)
-        make_xgm(2, nc.vector)
-        first(0)
-        transposes([("x", 3), ("x", 4)])
-        transposes([("x", 5)])
-        make_xgm(3, nc.vector)
-        times_first(0)
-        first(1)
-        quantise("x", 3)
-        quantise("x", 4)
+        for p in range(G):
+            quantise("x", p, (0,))
+        gate(0, 0)
+        first(0, 0)
+        make_xgm(0, 0)
+        make_xgm(1, 0)
+        make_xgm(2, 0)
+        for p, tag in ((0, "B"), (1, "T"), (2, "T")):
+            transposes("x", p, (1,), tag)
+        times_first(0, 0)
+        for p in range(G):
+            quantise("x", p, (1,))
+        make_xgm(0, 1)
+        gate(0, 1)
+        first(0, 1)
+        make_xgm(1, 1)
+        times_first(0, 1)
+        make_xgm(2, 1)
+        gate(1, 0)
+        first(1, 0)
+        transposes("x", 3)
+        transposes("x", 4)
         make_u(0)
-        quantise("x", 5)
-        times_first(1)
-        make_xgm(4, nc.vector)
-        transposes([("u", 0)])
-        first(2)
+        times_first(1, 0)
+        make_xgm(3)
+        gate(1, 1)
+        first(1, 1)
+        quantise("x", 3)
+        times_first(1, 1)
+        transposes("u", 0)
+        transposes("x", 5)
+        gate(2, 0)
+        first(2, 0)
+        quantise("x", 4)
         make_u(1)
+        quantise("x", 5)
+        times_first(2, 0)
+        make_xgm(4)
         quantise("u", 0)
-        times_first(2)
-        make_xgm(5, nc.vector)
+        gate(2, 1)
+        first(2, 1)
+        times_first(2, 1)
+        transposes("u", 1)
+        make_u(2)
+        quantise("u", 1)
 
-        for k in range(G, NB):
-            gate(k)
-            first(k)
-            make_u(k - 1)
-            for t in XGM_G.get(k, ()):
-                make_xgm(t, nc.gpsimd)
-            items = [("u", k - 1)]
-            if k == G:
-                items.insert(0, ("u", 1))
-            if k >= LAG + 2:
-                items.append(("r", k - LAG - 2))
-            if k + 3 < NB and k % G < 2:
-                items.append(("x", k + 3))
-            if k + 4 < NB and k % G == 1:
-                items.append(("x", k + 4))
-            if k >= LAG:
-                second(k - LAG)
-            transposes(items)
-            b = k - LAG - 1
-            if b >= 0:
-                times_second(b)
-            times_first(k)
-            if b >= 0:
-                add_first(b)
-            for t in XGM_AT.get(k, ()):
-                make_xgm(t, nc.vector)
-            for kind, t in items:
-                if kind != "u":
-                    quantise(kind, t)
-            if b >= 0:
-                result(b)
-            quantise("u", k - 1)
-            if k == G:
-                quantise("u", 1)
+        for p in range(3, STEPS):
+            gate(p, 0)
+            first(p, 0)
+            transposes("u", p - 1)
+            q = p - 4
+            if q >= 0:
+                times_second(q, 0)
+                times_second(q, 1)
+            times_first(p, 0)
+            gate(p, 1)
+            first(p, 1)
+            quantise("u", p - 1)
+            if q >= 0:
+                add_first(q)
+            if p == G:
+                make_xgm(5)
+            times_first(p, 1)
+            if q >= 0:
+                result(q)
+                round_result(q)
+            make_u(p)
+            if p < 5:
+                for t in range(2):
+                    second_start(p - 3, t)
+                    second_end(p - 3, t)
 
-        second_start(9, "G")
-        make_u(11)
-        second_start(10, "G")
-        transposes([("u", 11), ("r", 6)])
-        second(8)
-        second_start(11, "F")
-        times_second(7)
-        quantise("r", 6)
-        quantise("u", 11)
-        add_first(7)
-        second_end(9)
-        times_second(8)
-        result(7)
-        add_first(8)
-        second_end(10)
-        transposes([("r", 7)])
-        second_end(11)
-        times_second(9)
-        result(8)
-        times_second(10)
-        result(9)
-        transposes([("r", 8)])
-        quantise("r", 7)
-        times_second(11)
-        result(10)
-        transposes([("r", 9)])
-        result(11)
-        transposes([("r", 11)])
-        transposes([("r", 10)])
-        quantise("r", 8)
-        quantise("r", 9)
-        quantise("r", 10)
-        quantise("r", 11)
-
-        queues = (nc.sync, nc.scalar, nc.sync, nc.scalar)
-        for q in range(4):
-            queues[q].dma_start(
-                out=out_2[:, 4 * q : 4 * q + 4, :].rearrange("g q m -> q g m").bitcast(I32),
-                in_=rs[32 * q : 32 * q + 4, :, :].bitcast(I32),
-            )
+        second_start(2, 0)
+        second_end(2, 0)
+        second_start(2, 1)
+        second_end(2, 1)
+        second_start(4, 0, "G")
+        second_start(4, 1, "G")
+        transposes("u", 5)
+        transposes("r", 0)
+        times_second(2, 0)
+        times_second(2, 1)
+        quantise("u", 5)
+        second_start(3, 0)
+        second_end(3, 0)
+        second_start(3, 1)
+        second_end(3, 1)
+        add_first(2)
+        transposes("r", 1)
+        times_second(3, 0)
+        result(2)
+        round_result(2)
+        second_end(4, 0)
+        second_end(4, 1)
+        second_start(5, 0, "F")
+        second_end(5, 0)
+        second_start(5, 1, "F")
+        second_end(5, 1)
+        times_second(3, 1)
+        quantise("r", 0)
+        add_first(3)
+        times_second(4, 0)
+        result(3)
+        round_result(3)
+        transposes("r", 2)
+        times_second(4, 1)
+        quantise("r", 1)
+        times_second(5, 0)
+        result(4)
+        round_result(4)
+        transposes("r", 3)
+        times_second(5, 1)
+        quantise("r", 2)
+        result(5, 0)
+        round_result(5, 0)
+        transposes("r", 4)
+        result(5, 1, own_bf16=True)
+        quantise("r", 3)
+        transposes("r", 5)
+        quantise("r", 4)
+        quantise("r", 5)
+        store_scales()

from contextlib import ExitStack

import concourse.mybir as mybir
from concourse.masks import make_identity

B, D = 512, 1536
FLOPS = 3 * 2 * B * D * D

F32 = mybir.dt.float32
BF16 = mybir.dt.bfloat16
I32 = mybir.dt.int32
U32 = mybir.dt.uint32
U8 = mybir.dt.uint8
FP8X4 = mybir.dt.float8_e4m3fn_x4
FP4X4 = mybir.dt.float4_e2m1fn_x4
ALU = mybir.AluOpType
ACT = mybir.ActivationFunctionType

P = 128
G = D // 512
TILES = B // P
BLK = 512
HALVES = TILES // 2
STEPS = HALVES * G
REPEAT = 2


def tile_gateddeepcrosstwolayer_x2_kernel(
    tc, x, wg_words, wg_scales, wc1_words, wc1_scales, gm, wc2_words, wc2_scales, out_0, out_1, out_2
):
    nc = tc.nc
    with ExitStack() as ctx:
        keep = ctx.enter_context(tc.tile_pool(name="keep", bufs=1))
        work = ctx.enter_context(tc.tile_pool(name="work", bufs=3))
        psum = ctx.enter_context(tc.psum_pool(name="psum", bufs=2))
        ctx.enter_context(tc.manual_schedule())

        gm_rows = keep.tile([P, P], BF16, name="gm_rows", align_bytes=64)
        nc.vector.memset(gm_rows[:], 0.0)
        nc.gpsimd.dma_start(out=gm_rows[: D // P, :], in_=gm.rearrange("(c q) -> c q", q=P))
        ident = keep.tile([P, P], F32, name="ident")
        make_identity(nc, ident[:])
        warm = keep.tile([P, 1], F32, name="warm")
        nc.vector.memset(warm[:], 0.0)
        nc.scalar.activation(out=warm[:], in_=warm[:], func=ACT.Sigmoid)

        def scale_plane(name):
            t = keep.tile([P, G, D], U8, name=name, align_bytes=64)
            nc.vector.memset(t[:].rearrange("p g n -> p (g n)").bitcast(I32), 0)
            return t

        sg = scale_plane("sg")
        sc1 = scale_plane("sc1")
        sc2 = scale_plane("sc2")
        ident16 = keep.tile([P, P], BF16, name="ident16")
        nc.vector.tensor_copy(out=ident16[:], in_=ident[:])

        def load_scales(t, scales):
            for r in range(4):
                nc.sync.dma_start(
                    out=t[r:P:32, :, :].bitcast(I32),
                    in_=scales[:, r:16:4, :].rearrange("g q n -> q g n").bitcast(I32),
                )

        x_sb = keep.tile([P, TILES, D], BF16, name="x_sb", align_bytes=64)

        def load_x(i):
            nc.sync.dma_start(out=x_sb[:, i, :], in_=x[P * i : P * (i + 1), :])

        def load_w(name, words, j0, count):
            t = keep.tile([P, G, 2 * BLK * count], U8, name="%s_%d" % (name, j0), align_bytes=64)
            nc.sync.dma_start(
                out=t[:].bitcast(I32),
                in_=words[:, :, 2 * BLK * j0 : 2 * BLK * (j0 + count)].rearrange("g p n -> p g n").bitcast(I32),
            )
            return [(t, c) for c in range(count)]

        load_x(0)
        wg = load_w("wg", wg_words, 0, 1)
        load_scales(sg, wg_scales)
        load_scales(sc1, wc1_scales)
        wc1 = load_w("wc1", wc1_words, 0, 1)
        load_x(1)
        wg += load_w("wg", wg_words, 1, 1)
        wc1 += load_w("wc1", wc1_words, 1, 1)
        load_x(2)
        load_x(3)
        wg += load_w("wg", wg_words, 2, 1)
        wc1 += load_w("wc1", wc1_words, 2, 1)
        load_scales(sc2, wc2_scales)
        wc2 = load_w("wc2", wc2_words, 0, 3)

        xc, uc, rc = [keep.tile([P, G, B], U32, name=n, align_bytes=64) for n in ("xc", "uc", "rc")]
        xs, us, rs = [keep.tile([P, G, B], U8, name=n, align_bytes=64) for n in ("xs", "us", "rs")]
        gm_sb = keep.tile([P, D], BF16, name="gm_sb", align_bytes=64)

        def spread_gm_columns():
            bank = psum.tile([P, P], BF16, name="gbank", tag="F")
            nc.tensor.transpose(bank[:], gm_rows[:], ident16[:])
            gm_cols = keep.tile([P, P], BF16, name="gm_cols")
            nc.scalar.copy(out=gm_cols[:], in_=bank[:])
            return gm_cols

        def spread_gm(gm_cols):
            for first_col, count in ((0, 8), (8, 4)):
                bank = psum.tile([P, 8 * P], BF16, name="gbank", tag="T")
                for c in range(count):
                    nc.tensor.transpose(
                        bank[:, c * P : (c + 1) * P],
                        gm_cols[:, first_col + c : first_col + c + 1].to_broadcast([P, P]),
                        ident16[:],
                    )
                nc.scalar.copy(
                    out=gm_sb[:, first_col * P : (first_col + count) * P], in_=bank[:, : count * P]
                )

        gate_bank, first_bank, second_bank = {}, {}, {}
        sig, m, u_sb, m2, r_sb, rb, xgm, grouped = {}, {}, {}, {}, {}, {}, {}, {}

        def x_of(p, t=None):
            h, j = divmod(p, G)
            c = slice(BLK * j, BLK * (j + 1))
            return x_sb[:, 2 * h : 2 * h + 2, c] if t is None else x_sb[:, 2 * h + t, c]

        def mm(out, codes, scales, p, t, w, ws, start, stop):
            h, j = divmod(p, G)
            tok = slice(P * (2 * h + t), P * (2 * h + t + 1))
            tile, c = w[j]
            for g in range(G):
                nc.tensor.matmul_mx(
                    out=out[:],
                    lhsT=codes[:, g, tok].bitcast(FP8X4),
                    lhsT_scale=scales[:, g, tok],
                    rhs=tile[:, g, 2 * BLK * c : 2 * BLK * (c + 1)].bitcast(FP4X4),
                    rhs_scale=ws[:, g, BLK * j : BLK * (j + 1)],
                    start=start and g == 0,
                    stop=stop and g == G - 1,
                )

        def gate(p, t):
            gate_bank[p, t] = psum.tile([P, BLK], F32, name="gb", tag="G")
            mm(gate_bank[p, t], xc, xs, p, t, wg, sg, True, True)
            if t == 0:
                sig[p] = work.tile([P, 2, BLK], F32, name="sig", tag="sig", bufs=6)
            nc.scalar.activation(out=sig[p][:, t, :], in_=gate_bank[p, t][:], func=ACT.Sigmoid)

        def first(p, t):
            first_bank[p, t] = psum.tile([P, BLK], F32, name="fb", tag="F")
            mm(first_bank[p, t], xc, xs, p, t, wc1, sc1, True, True)

        def make_xgm(p, t=None, engine=None):
            j = p % G
            if p not in xgm:
                xgm[p] = work.tile([P, 2, BLK], F32, name="xgm", tag="xgm", bufs=6)
            g = gm_sb[:, BLK * j : BLK * (j + 1)]
            (engine or nc.vector).tensor_tensor(
                out=xgm[p][:] if t is None else xgm[p][:, t, :],
                in0=x_of(p, t),
                in1=g.unsqueeze(1).to_broadcast([P, 2, BLK]) if t is None else g,
                op=ALU.mult,
            )

        def times_first(p, t):
            if t == 0:
                m[p] = work.tile([P, 2, BLK], F32, name="m", tag="m", bufs=5)
            nc.vector.tensor_tensor(out=m[p][:, t, :], in0=first_bank[p, t][:], in1=sig[p][:, t, :], op=ALU.mult)

        def make_u(p):
            u_sb[p] = work.tile([P, 2, BLK], BF16, name="u", tag="u", bufs=2)
            nc.vector.scalar_tensor_tensor(
                out=u_sb[p][:], in0=m[p][:], scalar=1.0, in1=xgm[p][:], op0=ALU.add, op1=ALU.mult
            )

        def transposes(kind, p, tiles=(0, 1), tag="T", copy=nc.scalar.copy):
            bank = psum.tile([P, 4 * P], F32, name="bank", tag=tag)
            n = len(tiles)
            for k, t in enumerate(tiles):
                src = x_of(p, t) if kind == "x" else (u_sb if kind == "u" else rb)[p][:, t, :]
                for w in range(2):
                    col = (2 * k + w) * P
                    nc.tensor.transpose(bank[:, col : col + P], src.bitcast(F32)[:, w : 2 * P : 2], ident[:])
            g = work.tile([P, 8 * P], BF16, name="grouped", tag="grouped", bufs=5, align_bytes=64)
            copy(
                out=g[:, : 4 * P * n].bitcast(F32).rearrange("p (k r u) -> p k r u", k=n, u=2),
                in_=bank[:, : 2 * P * n].rearrange("p (k u r) -> p k r u", k=n, u=2),
            )
            grouped[kind, p, tiles] = g

        def quantise(kind, p, tiles=(0, 1)):
            h, j = divmod(p, G)
            codes, scales = {"x": (xc, xs), "u": (uc, us), "r": (rc, rs)}[kind]
            n = len(tiles)
            tok = slice(P * (2 * h + tiles[0]), P * (2 * h + tiles[0] + n))
            nc.vector.quantize_mx(
                out=codes[:, j, tok].bitcast(FP8X4),
                scales=scales[:, j, tok],
                in_=grouped[kind, p, tiles][:, : 4 * P * n],
            )
            if kind == "r":
                nc.sync.dma_start(
                    out=out_1[j, :, tok, :].rearrange("p m t -> p (m t)").bitcast(I32),
                    in_=rc[:, j, tok].bitcast(I32),
                )

        def store_scales():
            queues = (nc.sync, nc.scalar)
            for q in range(4):
                queues[q % 2].dma_start(
                    out=out_2[:, 4 * q : 4 * q + 4, :].rearrange("g q m -> q g m").bitcast(I32),
                    in_=rs[32 * q : 32 * q + 4, :, :].bitcast(I32),
                )

        def repeated(p):
            return p >= STEPS - REPEAT

        def second_start(p, t, tag="B"):
            second_bank[p, t] = psum.tile([P, BLK], F32, name="bb", tag=tag)
            if repeated(p):
                mm(second_bank[p, t], xc, xs, p, t, wc1, sc1, True, False)

        def second_end(p, t):
            mm(second_bank[p, t], uc, us, p, t, wc2, sc2, not repeated(p), True)

        def times_second(p, t):
            if t == 0:
                m2[p] = work.tile([P, 2, BLK], F32, name="m2", tag="m2", bufs=3)
            nc.vector.tensor_tensor(out=m2[p][:, t, :], in0=second_bank[p, t][:], in1=sig[p][:, t, :], op=ALU.mult)

        def add_first(p):
            if not repeated(p):
                nc.vector.tensor_tensor(out=m2[p][:], in0=m2[p][:], in1=m[p][:], op=ALU.add)

        def result(p, t=None, own_bf16=False):
            h, j = divmod(p, G)
            if p not in r_sb:
                r_sb[p] = work.tile([P, 2, BLK], F32, name="r", tag="r", bufs=3)
                rb[p] = work.tile([P, 2, BLK], BF16, name="rb", tag="rb", bufs=3)
            part = (lambda a: a[:]) if t is None else (lambda a: a[:, t, :])
            for a in [rb[p], r_sb[p]] if own_bf16 else [r_sb[p]]:
                nc.vector.scalar_tensor_tensor(
                    out=part(a), in0=part(m2[p]), scalar=1.0, in1=x_of(p, t), op0=ALU.add, op1=ALU.mult
                )
            c = slice(BLK * j, BLK * (j + 1))
            if t is None:
                dst = out_0[2 * P * h : 2 * P * (h + 1), c].rearrange("(t p) n -> p t n", t=2)
            else:
                dst = out_0[P * (2 * h + t) : P * (2 * h + t + 1), c]
            nc.sync.dma_start(out=dst, in_=part(r_sb[p]))

        def round_result(p, t=None):
            part = (lambda a: a[:]) if t is None else (lambda a: a[:, t, :])
            nc.scalar.copy(out=part(rb[p]), in_=part(r_sb[p]))

        gm_cols = spread_gm_columns()
        for p, tag, copy in ((0, "B", nc.vector.tensor_copy), (1, "G", nc.scalar.copy), (2, "B", nc.vector.tensor_copy)):
            transposes("x", p, (0,), tag, copy)
        spread_gm(gm_cols)
        for p in range(G):
            quantise("x", p, (0,))
        gate(0, 0)
        first(0, 0)
        make_xgm(0, 0)
        make_xgm(1, 0)
        make_xgm(2, 0)
        for p, tag in ((0, "B"), (1, "T"), (2, "T")):
            transposes("x", p, (1,), tag)
        times_first(0, 0)
        for p in range(G):
            quantise("x", p, (1,))
        make_xgm(0, 1)
        gate(0, 1)
        first(0, 1)
        make_xgm(1, 1)
        times_first(0, 1)
        make_xgm(2, 1)
        gate(1, 0)
        first(1, 0)
        transposes("x", 3)
        transposes("x", 4)
        make_u(0)
        times_first(1, 0)
        make_xgm(3)
        gate(1, 1)
        first(1, 1)
        quantise("x", 3)
        times_first(1, 1)
        transposes("u", 0)
        transposes("x", 5)
        gate(2, 0)
        first(2, 0)
        quantise("x", 4)
        make_u(1)
        quantise("x", 5)
        times_first(2, 0)
        make_xgm(4)
        quantise("u", 0)
        gate(2, 1)
        first(2, 1)
        times_first(2, 1)
        transposes("u", 1)
        make_u(2)
        quantise("u", 1)

        for p in range(3, STEPS):
            gate(p, 0)
            first(p, 0)
            transposes("u", p - 1)
            q = p - 4
            if q >= 0:
                times_second(q, 0)
                times_second(q, 1)
            times_first(p, 0)
            gate(p, 1)
            first(p, 1)
            quantise("u", p - 1)
            if q >= 0:
                add_first(q)
            if p == G:
                make_xgm(5)
            times_first(p, 1)
            if q >= 0:
                result(q)
                round_result(q)
            make_u(p)
            if p < 5:
                for t in range(2):
                    second_start(p - 3, t)
                    second_end(p - 3, t)

        second_start(2, 0)
        second_end(2, 0)
        second_start(2, 1)
        second_end(2, 1)
        second_start(4, 0, "G")
        second_start(4, 1, "G")
        transposes("u", 5)
        transposes("r", 0)
        times_second(2, 0)
        times_second(2, 1)
        quantise("u", 5)
        second_start(3, 0)
        second_end(3, 0)
        second_start(3, 1)
        second_end(3, 1)
        add_first(2)
        transposes("r", 1)
        times_second(3, 0)
        result(2)
        round_result(2)
        second_end(4, 0)
        second_end(4, 1)
        second_start(5, 0, "F")
        second_end(5, 0)
        second_start(5, 1, "F")
        second_end(5, 1)
        times_second(3, 1)
        quantise("r", 0)
        add_first(3)
        times_second(4, 0)
        result(3)
        round_result(3)
        transposes("r", 2)
        times_second(4, 1)
        quantise("r", 1)
        times_second(5, 0)
        result(4)
        round_result(4)
        transposes("r", 3)
        times_second(5, 1)
        quantise("r", 2)
        result(5, 0)
        round_result(5, 0)
        transposes("r", 4)
        result(5, 1, own_bf16=True)
        quantise("r", 3)
        transposes("r", 5)
        quantise("r", 4)
        quantise("r", 5)
        store_scales()
